import numpy as np
import ml_dtypes


def mxq(x, axis, fmt="e4m3"):
    dtype, down = {"e4m3": (ml_dtypes.float8_e4m3fn, 7), "e5m2": (ml_dtypes.float8_e5m2, 14)}[fmt]
    v = np.moveaxis(np.asarray(x, np.float32).astype(ml_dtypes.bfloat16).astype(np.float64), axis, -1)
    blocks = v.reshape(v.shape[:-1] + (-1, 32))
    amax = np.abs(blocks).max(-1, keepdims=True)
    byte = np.maximum(np.where(amax > 0, np.frexp(amax)[1] - 1 + 127, 0) - down, 1)
    scale = np.exp2(byte - 127.0)
    codes = (blocks / scale).astype(np.float32).astype(dtype).astype(np.float64)
    return np.moveaxis((codes * scale).reshape(v.shape), -1, axis)


WIDE = False


def mx_kscale(k):
    if not WIDE:
        return np.ones(k)
    levels = np.array([30, -30])
    if k % 512:
        return np.exp2(np.random.permutation(np.resize(levels, k // 32))).repeat(32)
    a = np.empty((k // 512, 16))
    for p in range(k // 512):
        a[p, :8] = np.random.permutation(np.resize(levels, 8))
        for g in range(8):
            far = levels[np.abs(levels - a[p, g]) >= 10]
            a[p, g + 8] = far[np.random.randint(len(far))]
    return np.exp2(a.ravel()).repeat(32)


def f64(x):
    return np.asarray(x).astype(np.float64)


def striped(idx):
    return np.tile(np.asarray(idx).reshape(-1, 16).T, (8, 1)).astype(np.uint16)


def unstriped(offs):
    return offs[:16].T.reshape(-1).astype(np.int64)


E2M1 = np.array([0.0, 0.5, 1.0, 1.5, 2.0, 3.0, 4.0, 6.0, -0.0, -0.5, -1.0, -1.5, -2.0, -3.0, -4.0, -6.0])


def pack_weight(w, fmt):
    k, n = w.shape
    w = f64(np.asarray(w, np.float32).astype(ml_dtypes.bfloat16)).reshape(k // 32, 32, n)
    amax = np.abs(w).max(1)
    if fmt in ("e4m3", "e5m2"):
        byte = np.frexp(amax)[1] - 1 + 127 - (7 if fmt == "e4m3" else 14)
    else:
        mant, ex = np.frexp(amax / 6.0)
        byte = np.where(mant > 0.5, ex, ex - 1) + 127
    byte = np.clip(np.where(amax > 0, byte, 1), 1, 254)
    scaled = (w * np.exp2(127.0 - byte)[:, None, :]).reshape(k, n).astype(np.float32)
    by_word = np.ascontiguousarray(scaled.reshape(k // 512, 128, 4, n).transpose(0, 1, 3, 2))
    if fmt in ("e4m3", "e5m2"):
        words = by_word.astype(ml_dtypes.float8_e4m3fn if fmt == "e4m3" else ml_dtypes.float8_e5m2).view(np.uint8)
    else:
        c = by_word.astype(ml_dtypes.float4_e2m1fn).view(np.uint8) & 0xF
        words = (c[..., 0::2] | (c[..., 1::2] << 4)).reshape(k // 512, 128, 2 * n)
    return np.ascontiguousarray(words), np.ascontiguousarray(byte.astype(np.uint8).reshape(k // 512, 16, n))


def unpack_weight(words, scales, fmt):
    g, _, n = scales.shape
    words = np.ascontiguousarray(words).reshape(g, 128, n, -1)
    if fmt in ("e4m3", "e5m2"):
        vals = words.view(ml_dtypes.float8_e4m3fn if fmt == "e4m3" else ml_dtypes.float8_e5m2).astype(np.float64)
    else:
        nib = np.empty((g, 128, n, 4), np.uint8)
        nib[..., 0::2] = words & 0xF
        nib[..., 1::2] = words >> 4
        vals = E2M1[nib]
    vals = vals * np.repeat(np.exp2(scales.astype(np.float64) - 127.0), 8, axis=1)[..., None]
    return vals.transpose(0, 1, 3, 2).reshape(g * 512, n)


K, T, J, R, C, N, E = 512, 2048, 256, 512, 512, 256, 1024


def setup_inputs():
    n = np.random.standard_normal
    idx = np.random.permutation(T)[:J]
    idx2 = np.random.permutation(T)[:J]
    idx3 = np.random.permutation(C)[:J]
    idx4 = np.random.permutation(C)[:J]
    idx5 = np.random.permutation(E)[:J]
    fk = mx_kscale(K)
    fr = mx_kscale(R)
    xtp = pack_weight(n((K, T)) / fk[:, None], "e5m2")
    wp = pack_weight(n((K, R)) * 1 / np.sqrt(K) * fk[:, None] * fr, "e2m1")
    w2p = pack_weight(n((K, R)) * 1 / np.sqrt(K) * fk[:, None] * fr, "e4m3")
    wbp = pack_weight(n((R, N)) * 1 / np.sqrt(R) / fr[:, None], "e2m1")
    return {
        "xt_words": xtp[0],
        "xt_scales": xtp[1],
        "w_words": wp[0],
        "w_scales": wp[1],
        "w2_words": w2p[0],
        "w2_scales": w2p[1],
        "wb_words": wbp[0],
        "wb_scales": wbp[1],
        "tz": (n((N, E))).astype(np.float32),
        "offs": striped(idx),
        "offs2": striped(idx2),
        "offs3": striped(idx3),
        "offs4": striped(idx4),
        "offs5": striped(idx5),
    }


def reference(xt_words, xt_scales, w_words, w_scales, w2_words, w2_scales, wb_words, wb_scales, tz, offs, offs2, offs3, offs4, offs5):
    idx = unstriped(offs)
    idx2 = unstriped(offs2)
    idx3 = unstriped(offs3)
    idx4 = unstriped(offs4)
    idx5 = unstriped(offs5)
    xtu = unpack_weight(xt_words, xt_scales, "e5m2")
    wu = unpack_weight(w_words, w_scales, "e2m1")
    w2u = unpack_weight(w2_words, w2_scales, "e4m3")
    wbu = unpack_weight(wb_words, wb_scales, "e2m1")
    xtidxg = xtu[:, idx]
    a = wu.T @ xtidxg
    xtidx2g = xtu[:, idx2]
    b = w2u.T @ xtidx2g
    pw = np.zeros((R, C))
    pw[:, idx3] = a
    hid = np.abs(pw[:, idx4] - b)
    hidq = mxq(hid, 0, "e4m3")
    p = wbu.T @ hidq
    y = p + f64(tz)[:, idx5]
    return y

@@ -1,0 +1,183 @@
+from contextlib import ExitStack
+
+import concourse.mybir as mybir
+
+K, T, J, R, C, N, E = 512, 2048, 256, 512, 512, 256, 1024
+FLOPS = 2 * K * R * J * 2 + 2 * R * N * J
+
+F32 = mybir.dt.float32
+BF16 = mybir.dt.bfloat16
+I32 = mybir.dt.int32
+U32 = mybir.dt.uint32
+U16 = mybir.dt.uint16
+U8 = mybir.dt.uint8
+E4M3X4 = mybir.dt.float8_e4m3fn_x4
+E5M2X4 = mybir.dt.float8_e5m2_x4
+E2M1X4 = mybir.dt.float4_e2m1fn_x4
+ACT = mybir.ActivationFunctionType
+ALU = mybir.AluOpType
+
+P = 128
+PACK = 4
+HALVES = 2
+JH = J // HALVES
+LIST_COLS = J // 16
+NT = N // P
+
+
+def tile_list_ahead_board_one_tabled_kernel(
+    tc, xt_words, xt_scales, w_words, w_scales, w2_words, w2_scales, wb_words, wb_scales,
+    tz, offs, offs2, offs3, offs4, offs5, out,
+):
+    nc = tc.nc
+    with ExitStack() as ctx:
+        sb = ctx.enter_context(tc.tile_pool(name="sb", bufs=1))
+        ps = ctx.enter_context(tc.psum_pool(name="ps", bufs=1))
+
+        def tile(name, shape, dtype):
+            return sb.tile(shape, dtype, name=name, align_bytes=64)
+
+        def load_list(name, src):
+            lst = tile(name, [P, LIST_COLS], U16)
+            nc.sync.dma_start(lst[:], src)
+            return lst
+
+        def zeroed_plane(name, width, engine):
+            plane = tile(name, [P, width], U8)
+            engine.memset(plane[:].bitcast(I32), 0)
+            return plane
+
+        def load_plane(plane, src, queue):
+            for q in range(4):
+                queue.dma_start(plane[32 * q : 32 * q + 4, :].bitcast(I32), src[0, 4 * q : 4 * q + 4, :].bitcast(I32))
+
+        def load_words(name, src, words):
+            codes = tile(name, [P, words], I32)
+            nc.sync.dma_start(codes[:], src.bitcast(I32))
+            return codes
+
+        def gather(engine, dst, window, lst):
+            if engine is nc.vector:
+                nc.vector.tensor_copy(dst, window.indirect(lst))
+            else:
+                nc.scalar.activation(dst, window.indirect(lst), ACT.Copy)
+
+        def scatter(engine, window, lst, src):
+            if engine is nc.vector:
+                nc.vector.tensor_copy(window.indirect(lst), src)
+            else:
+                nc.scalar.activation(window.indirect(lst), src, ACT.Copy)
+
+        ws_raw = zeroed_plane("ws_raw", R, nc.vector)
+        xs = zeroed_plane("xs", T, nc.vector)
+        wbs = zeroed_plane("wbs", N, nc.gpsimd)
+        w2s_raw = zeroed_plane("w2s_raw", R, nc.gpsimd)
+        board = [tile("board%d" % t, [P, C], F32) for t in range(PACK)]
+        for t in range(PACK):
+            nc.vector.memset(board[t][:], 0.0)
+
+        l1 = load_list("l1", offs)
+        w_raw = load_words("w_raw", w_words[0], R // 2)
+        load_plane(ws_raw, w_scales, nc.sync)
+        x_words = load_words("x_words", xt_words[0].rearrange("p c b -> p (c b)"), T)
+        load_plane(xs, xt_scales, nc.sync)
+        l2 = load_list("l2", offs2)
+        l5 = load_list("l5", offs5)
+        tz_sb = [tile("tz%d" % u, [P, E], F32) for u in range(NT)]
+        nc.sync.dma_start(tz_sb[0][:], tz[0:P, :])
+        l3 = load_list("l3", offs3)
+        w2_raw = load_words("w2_raw", w2_words[0].rearrange("p c b -> p (c b)"), R)
+        load_plane(w2s_raw, w2_scales, nc.sync)
+        l4 = load_list("l4", offs4)
+        nc.sync.dma_start(tz_sb[1][:], tz[P : 2 * P, :])
+        wb_codes = load_words("wb_codes", wb_words[0], N // 2)
+        load_plane(wbs, wb_scales, nc.gpsimd)
+
+        def deal(engine, name, raw, dtype):
+            dealt = tile(name, [P, R], dtype)
+            engine.tensor_copy(dealt[:].rearrange("p (t m) -> p t m", t=PACK), raw.rearrange("p (m t) -> p t m", t=PACK))
+            return dealt
+
+        w_codes = deal(nc.vector, "w_codes", w_raw[:].bitcast(U16), U16)
+        ws = deal(nc.vector, "ws", ws_raw[:], U8)
+
+        def pick_tokens(name, lst):
+            words = tile(name + "_words", [P, J], U32)
+            scales = tile(name + "_scales", [P, J], U8)
+            nc.vector.tensor_copy(words[:], x_words[:].bitcast(U32).indirect(lst[:]))
+            nc.vector.tensor_copy(scales[:], xs[:].indirect(lst[:]))
+            return words, scales
+
+        x1_words, x1_scales = pick_tokens("x1", l1)
+        x2_words, x2_scales = pick_tokens("x2", l2)
+
+        tz_pick = tile("tz_pick", [P, NT, J], F32)
+        gather(nc.scalar, tz_pick[:, 0, :], tz_sb[0][:], l5[:])
+
+        owner = [nc.vector, nc.vector, nc.scalar, nc.scalar]
+        a_sb = [tile("a%d" % t, [P, J], F32) for t in range(PACK)]
+        for t in (0, 2, 1, 3):
+            a_ps = ps.tile([P, J], F32, name="a_ps%d" % t)
+            cols = slice(t * P, (t + 1) * P)
+            nc.tensor.matmul_mx(
+                out=a_ps[:],
+                lhsT=w_codes[:].bitcast(U8)[:, 2 * t * P : 2 * (t + 1) * P].bitcast(E2M1X4), lhsT_scale=ws[:, cols],
+                rhs=x1_words[:].bitcast(E5M2X4), rhs_scale=x1_scales[:],
+                start=True, stop=True,
+            )
+            nc.scalar.activation(a_sb[t][:], a_ps[:], ACT.Copy)
+        for t in (0, 2, 1, 3):
+            scatter(owner[t], board[t][:], l3[:], a_sb[t][:])
+
+        w2_codes = deal(nc.gpsimd, "w2_codes", w2_raw[:], I32)
+        w2s = deal(nc.gpsimd, "w2s", w2s_raw[:], U8)
+        b_ps = [ps.tile([P, PACK, JH], F32, name="b_ps%d" % h) for h in range(HALVES)]
+        for h in range(HALVES):
+            slots = slice(h * JH, (h + 1) * JH)
+            for t in range(PACK):
+                cols = slice(t * P, (t + 1) * P)
+                nc.tensor.matmul_mx(
+                    out=b_ps[h][:, t, :],
+                    lhsT=w2_codes[:, cols].bitcast(E4M3X4), lhsT_scale=w2s[:, cols],
+                    rhs=x2_words[:, slots].bitcast(E5M2X4), rhs_scale=x2_scales[:, slots],
+                    start=True, stop=True,
+                )
+
+        picked = [tile("picked%d" % h, [P, PACK, JH], F32) for h in range(HALVES)]
+        for h in range(HALVES):
+            lcols = slice(h * LIST_COLS // HALVES, (h + 1) * LIST_COLS // HALVES)
+            for t in range(PACK):
+                gather(owner[t], picked[h][:, t, :], board[t][:], l4[:, lcols])
+
+        hid = []
+        for h in range(HALVES):
+            diff = tile("diff%d" % h, [P, PACK, JH], F32)
+            nc.vector.tensor_tensor(diff[:], picked[h][:], b_ps[h][:], ALU.subtract)
+            hid_h = tile("hid%d" % h, [P, JH, PACK], BF16)
+            nc.scalar.activation(hid_h[:], diff[:].rearrange("p t j -> p j t"), ACT.Abs)
+            hid.append(hid_h)
+
+        gather(nc.vector, tz_pick[:, 1, :], tz_sb[1][:], l5[:])
+
+        p_ps = []
+        for h in range(HALVES):
+            codes = tile("hid_codes%d" % h, [P, JH], U32)
+            scales = tile("hid_scales%d" % h, [P, JH], U8)
+            nc.vector.quantize_mx(out=codes[:].bitcast(E4M3X4), scales=scales[:], in_=hid[h][:].rearrange("p j t -> p (j t)"))
+            p_h = ps.tile([P, NT, JH], F32, name="p_ps%d" % h)
+            for u in range(NT):
+                nc.tensor.matmul_mx(
+                    out=p_h[:, u, :],
+                    lhsT=wb_codes[:].bitcast(U8)[:, 2 * u * P : 2 * (u + 1) * P].bitcast(E2M1X4),
+                    lhsT_scale=wbs[:, u * P : (u + 1) * P],
+                    rhs=codes[:].bitcast(E4M3X4), rhs_scale=scales[:],
+                    start=True, stop=True,
+                )
+            p_ps.append(p_h)
+
+        out_rows = out.rearrange("(u p) j -> p u j", p=P)
+        for h in range(HALVES):
+            slots = slice(h * JH, (h + 1) * JH)
+            y = tile("y%d" % h, [P, NT, JH], F32)
+            nc.vector.tensor_tensor(y[:], tz_pick[:, :, slots], p_ps[h][:], ALU.add)
+            nc.sync.dma_start(out_rows[:, :, slots], y[:])

@@ -47,13 +47,22 @@ def tile_list_ahead_board_one_tabled_kernel(
             engine.memset(plane[:].bitcast(I32), 0)
             return plane
 
-        def load_plane(plane, src, queue):
+        def load_plane(plane, src, queues):
             for q in range(4):
-                queue.dma_start(plane[32 * q : 32 * q + 4, :].bitcast(I32), src[0, 4 * q : 4 * q + 4, :].bitcast(I32))
+                queues[q].dma_start(plane[32 * q : 32 * q + 4, :].bitcast(I32), src[0, 4 * q : 4 * q + 4, :].bitcast(I32))
 
-        def load_words(name, src, words):
+        def load_full_plane(name, src, width, queues):
+            plane = tile(name, [P, width], U8)
+            for q in range(4):
+                rows = src[0, 4 * q : 4 * q + 4, :].bitcast(I32)
+                queues[q].dma_start(
+                    plane[32 * q : 32 * (q + 1), :].bitcast(I32), rows.unsqueeze(0).broadcast_to([8, 4, width // 4])
+                )
+            return plane
+
+        def load_words(name, src, words, queue=nc.sync):
             codes = tile(name, [P, words], I32)
-            nc.sync.dma_start(codes[:], src.bitcast(I32))
+            queue.dma_start(codes[:], src.bitcast(I32))
             return codes
 
         def gather(engine, dst, window, lst):
@@ -68,54 +77,52 @@ def tile_list_ahead_board_one_tabled_kernel(
             else:
                 nc.scalar.activation(window.indirect(lst), src, ACT.Copy)
 
-        ws_raw = zeroed_plane("ws_raw", R, nc.vector)
         xs = zeroed_plane("xs", T, nc.vector)
-        wbs = zeroed_plane("wbs", N, nc.gpsimd)
-        w2s_raw = zeroed_plane("w2s_raw", R, nc.gpsimd)
         board = [tile("board%d" % t, [P, C], F32) for t in range(PACK)]
         for t in range(PACK):
             nc.vector.memset(board[t][:], 0.0)
 
         l1 = load_list("l1", offs)
-        w_raw = load_words("w_raw", w_words[0], R // 2)
-        load_plane(ws_raw, w_scales, nc.sync)
-        x_words = load_words("x_words", xt_words[0].rearrange("p c b -> p (c b)"), T)
-        load_plane(xs, xt_scales, nc.sync)
         l2 = load_list("l2", offs2)
-        l5 = load_list("l5", offs5)
-        tz_sb = [tile("tz%d" % u, [P, E], F32) for u in range(NT)]
-        nc.sync.dma_start(tz_sb[0][:], tz[0:P, :])
+        w_raw = load_words("w_raw", w_words[0], R // 2, nc.scalar)
+        load_plane(xs, xt_scales, [nc.sync, nc.scalar] * 2)
+        x_words = load_words("x_words", xt_words[0].rearrange("p c b -> p (c b)"), T)
         l3 = load_list("l3", offs3)
+        ws_raw = load_full_plane("ws_raw", w_scales, R, [nc.sync] * 4)
         w2_raw = load_words("w2_raw", w2_words[0].rearrange("p c b -> p (c b)"), R)
-        load_plane(w2s_raw, w2_scales, nc.sync)
+        w2s_raw = load_full_plane("w2s_raw", w2_scales, R, [nc.sync] * 4)
+        tz_sb = [tile("tz%d" % u, [P, E], F32) for u in range(NT)]
+        for u in range(NT):
+            nc.sync.dma_start(tz_sb[u][:], tz[u * P : (u + 1) * P, :])
         l4 = load_list("l4", offs4)
-        nc.sync.dma_start(tz_sb[1][:], tz[P : 2 * P, :])
         wb_codes = load_words("wb_codes", wb_words[0], N // 2)
-        load_plane(wbs, wb_scales, nc.gpsimd)
+        l5 = load_list("l5", offs5)
+        wbs = load_full_plane("wbs", wb_scales, N, [nc.sync] * 4)
 
         def deal(engine, name, raw, dtype):
             dealt = tile(name, [P, R], dtype)
-            engine.tensor_copy(dealt[:].rearrange("p (t m) -> p t m", t=PACK), raw.rearrange("p (m t) -> p t m", t=PACK))
+            engine(dealt[:].rearrange("p (t m) -> p t m", t=PACK), raw.rearrange("p (m t) -> p t m", t=PACK))
             return dealt
 
-        w_codes = deal(nc.vector, "w_codes", w_raw[:].bitcast(U16), U16)
-        ws = deal(nc.vector, "ws", ws_raw[:], U8)
+        def pick(name, window, lst, dtype):
+            picked_bytes = tile(name, [P, J], dtype)
+            nc.vector.tensor_copy(picked_bytes[:], window.indirect(lst[:]))
+            return picked_bytes
 
-        def pick_tokens(name, lst):
-            words = tile(name + "_words", [P, J], U32)
-            scales = tile(name + "_scales", [P, J], U8)
-            nc.vector.tensor_copy(words[:], x_words[:].bitcast(U32).indirect(lst[:]))
-            nc.vector.tensor_copy(scales[:], xs[:].indirect(lst[:]))
-            return words, scales
+        w_codes = deal(nc.vector.tensor_copy, "w_codes", w_raw[:].bitcast(U16), U16)
+        x1_scales = pick("x1_scales", xs[:], l1, U8)
+        x2_scales = pick("x2_scales", xs[:], l2, U8)
+        x1_words = pick("x1_words", x_words[:].bitcast(U32), l1, U32)
+        ws = tile("ws", [P, R], U8)
+        for t in (0, 2, 1, 3):
+            nc.vector.tensor_copy(ws[:, t * P : (t + 1) * P], ws_raw[:, t : R : PACK])
+        x2_words = pick("ws_raw", x_words[:].bitcast(U32), l2, U32)
 
-        x1_words, x1_scales = pick_tokens("x1", l1)
-        x2_words, x2_scales = pick_tokens("x2", l2)
-
-        tz_pick = tile("tz_pick", [P, NT, J], F32)
-        gather(nc.scalar, tz_pick[:, 0, :], tz_sb[0][:], l5[:])
+        w2_codes = deal(nc.gpsimd.tensor_copy, "w2_codes", w2_raw[:], I32)
+        w2s = deal(nc.gpsimd.tensor_copy, "w2s", w2s_raw[:], U8)
 
         owner = [nc.vector, nc.vector, nc.scalar, nc.scalar]
-        a_sb = [tile("a%d" % t, [P, J], F32) for t in range(PACK)]
+        a_sb = [tile("a%d" % t, [P, J], F32)[:] for t in range(PACK)]
         for t in (0, 2, 1, 3):
             a_ps = ps.tile([P, J], F32, name="a_ps%d" % t)
             cols = slice(t * P, (t + 1) * P)
@@ -125,12 +132,12 @@ def tile_list_ahead_board_one_tabled_kernel(
                 rhs=x1_words[:].bitcast(E5M2X4), rhs_scale=x1_scales[:],
                 start=True, stop=True,
             )
-            nc.scalar.activation(a_sb[t][:], a_ps[:], ACT.Copy)
-        for t in (0, 2, 1, 3):
-            scatter(owner[t], board[t][:], l3[:], a_sb[t][:])
+            if owner[t] is nc.vector:
+                nc.vector.tensor_copy(a_sb[t], a_ps[:])
+            else:
+                nc.scalar.activation(a_sb[t], a_ps[:], ACT.Copy)
+            scatter(owner[t], board[t][:], l3[:], a_sb[t])
 
-        w2_codes = deal(nc.gpsimd, "w2_codes", w2_raw[:], I32)
-        w2s = deal(nc.gpsimd, "w2s", w2s_raw[:], U8)
         b_ps = [ps.tile([P, PACK, JH], F32, name="b_ps%d" % h) for h in range(HALVES)]
         for h in range(HALVES):
             slots = slice(h * JH, (h + 1) * JH)
@@ -143,21 +150,21 @@ def tile_list_ahead_board_one_tabled_kernel(
                     start=True, stop=True,
                 )
 
-        picked = [tile("picked%d" % h, [P, PACK, JH], F32) for h in range(HALVES)]
-        for h in range(HALVES):
-            lcols = slice(h * LIST_COLS // HALVES, (h + 1) * LIST_COLS // HALVES)
-            for t in range(PACK):
-                gather(owner[t], picked[h][:, t, :], board[t][:], l4[:, lcols])
-
         hid = []
         for h in range(HALVES):
+            picked = tile("picked%d" % h, [P, PACK, JH], F32)
+            lcols = slice(h * LIST_COLS // HALVES, (h + 1) * LIST_COLS // HALVES)
+            for t in range(PACK):
+                gather(owner[t], picked[:, t, :], board[t][:], l4[:, lcols])
             diff = tile("diff%d" % h, [P, PACK, JH], F32)
-            nc.vector.tensor_tensor(diff[:], picked[h][:], b_ps[h][:], ALU.subtract)
-            hid_h = tile("hid%d" % h, [P, JH, PACK], BF16)
+            nc.vector.tensor_tensor(diff[:], picked[:], b_ps[h][:], ALU.subtract)
+            hid.append((diff, tile("hid%d" % h, [P, JH, PACK], BF16)))
+        tz_pick = tile("tz_pick", [P, NT, J], F32)
+        gather(nc.vector, tz_pick[:, 0, :], tz_sb[0][:], l5[:])
+        gather(nc.scalar, tz_pick[:, 1, :], tz_sb[1][:], l5[:])
+        for diff, hid_h in hid:
             nc.scalar.activation(hid_h[:], diff[:].rearrange("p t j -> p j t"), ACT.Abs)
-            hid.append(hid_h)
-
-        gather(nc.vector, tz_pick[:, 1, :], tz_sb[1][:], l5[:])
+        hid = [hid_h for diff, hid_h in hid]
 
         p_ps = []
         for h in range(HALVES):

@@ -163,7 +163,9 @@ def tile_list_ahead_board_one_tabled_kernel(
         gather(nc.vector, tz_pick[:, 0, :], tz_sb[0][:], l5[:])
         gather(nc.scalar, tz_pick[:, 1, :], tz_sb[1][:], l5[:])
         for diff, hid_h in hid:
-            nc.scalar.activation(hid_h[:], diff[:].rearrange("p t j -> p j t"), ACT.Abs)
+            nc.scalar.activation(
+                hid_h[:].rearrange("p (c i) t -> p c t i", i=4), diff[:].rearrange("p t (c i) -> p c t i", i=4), ACT.Abs
+            )
         hid = [hid_h for diff, hid_h in hid]
 
         p_ps = []
@@ -187,4 +189,5 @@ def tile_list_ahead_board_one_tabled_kernel(
             slots = slice(h * JH, (h + 1) * JH)
             y = tile("y%d" % h, [P, NT, JH], F32)
             nc.vector.tensor_tensor(y[:], tz_pick[:, :, slots], p_ps[h][:], ALU.add)
-            nc.sync.dma_start(out_rows[:, :, slots], y[:])
+            for u, queue in enumerate((nc.sync, nc.scalar)):
+                queue.dma_start(out_rows[:, u, slots], y[:, u, :])

from contextlib import ExitStack

import concourse.mybir as mybir

K, T, J, R, C, N, E = 512, 2048, 256, 512, 512, 256, 1024
FLOPS = 2 * K * R * J * 2 + 2 * R * N * J

F32 = mybir.dt.float32
BF16 = mybir.dt.bfloat16
I32 = mybir.dt.int32
U32 = mybir.dt.uint32
U16 = mybir.dt.uint16
U8 = mybir.dt.uint8
E4M3X4 = mybir.dt.float8_e4m3fn_x4
E5M2X4 = mybir.dt.float8_e5m2_x4
E2M1X4 = mybir.dt.float4_e2m1fn_x4
ACT = mybir.ActivationFunctionType
ALU = mybir.AluOpType

P = 128
PACK = 4
HALVES = 2
JH = J // HALVES
LIST_COLS = J // 16
NT = N // P


def tile_list_ahead_board_one_tabled_kernel(
    tc, xt_words, xt_scales, w_words, w_scales, w2_words, w2_scales, wb_words, wb_scales,
    tz, offs, offs2, offs3, offs4, offs5, out,
):
    nc = tc.nc
    with ExitStack() as ctx:
        sb = ctx.enter_context(tc.tile_pool(name="sb", bufs=1))
        ps = ctx.enter_context(tc.psum_pool(name="ps", bufs=1))

        def tile(name, shape, dtype):
            return sb.tile(shape, dtype, name=name, align_bytes=64)

        def load_list(name, src):
            lst = tile(name, [P, LIST_COLS], U16)
            nc.sync.dma_start(lst[:], src)
            return lst

        def zeroed_plane(name, width, engine):
            plane = tile(name, [P, width], U8)
            engine.memset(plane[:].bitcast(I32), 0)
            return plane

        def load_plane(plane, src, queues):
            for q in range(4):
                queues[q].dma_start(plane[32 * q : 32 * q + 4, :].bitcast(I32), src[0, 4 * q : 4 * q + 4, :].bitcast(I32))

        def load_full_plane(name, src, width, queues):
            plane = tile(name, [P, width], U8)
            for q in range(4):
                rows = src[0, 4 * q : 4 * q + 4, :].bitcast(I32)
                queues[q].dma_start(
                    plane[32 * q : 32 * (q + 1), :].bitcast(I32), rows.unsqueeze(0).broadcast_to([8, 4, width // 4])
                )
            return plane

        def load_words(name, src, words, queue=nc.sync):
            codes = tile(name, [P, words], I32)
            queue.dma_start(codes[:], src.bitcast(I32))
            return codes

        def gather(engine, dst, window, lst):
            if engine is nc.vector:
                nc.vector.tensor_copy(dst, window.indirect(lst))
            else:
                nc.scalar.activation(dst, window.indirect(lst), ACT.Copy)

        def scatter(engine, window, lst, src):
            if engine is nc.vector:
                nc.vector.tensor_copy(window.indirect(lst), src)
            else:
                nc.scalar.activation(window.indirect(lst), src, ACT.Copy)

        xs = zeroed_plane("xs", T, nc.vector)
        board = [tile("board%d" % t, [P, C], F32) for t in range(PACK)]
        for t in range(PACK):
            nc.vector.memset(board[t][:], 0.0)

        l1 = load_list("l1", offs)
        l2 = load_list("l2", offs2)
        w_raw = load_words("w_raw", w_words[0], R // 2, nc.scalar)
        load_plane(xs, xt_scales, [nc.sync, nc.scalar] * 2)
        x_words = load_words("x_words", xt_words[0].rearrange("p c b -> p (c b)"), T)
        l3 = load_list("l3", offs3)
        ws_raw = load_full_plane("ws_raw", w_scales, R, [nc.sync] * 4)
        w2_raw = load_words("w2_raw", w2_words[0].rearrange("p c b -> p (c b)"), R)
        w2s_raw = load_full_plane("w2s_raw", w2_scales, R, [nc.sync] * 4)
        tz_sb = [tile("tz%d" % u, [P, E], F32) for u in range(NT)]
        for u in range(NT):
            nc.sync.dma_start(tz_sb[u][:], tz[u * P : (u + 1) * P, :])
        l4 = load_list("l4", offs4)
        wb_codes = load_words("wb_codes", wb_words[0], N // 2)
        l5 = load_list("l5", offs5)
        wbs = load_full_plane("wbs", wb_scales, N, [nc.sync] * 4)

        def deal(engine, name, raw, dtype):
            dealt = tile(name, [P, R], dtype)
            engine(dealt[:].rearrange("p (t m) -> p t m", t=PACK), raw.rearrange("p (m t) -> p t m", t=PACK))
            return dealt

        def pick(name, window, lst, dtype):
            picked_bytes = tile(name, [P, J], dtype)
            nc.vector.tensor_copy(picked_bytes[:], window.indirect(lst[:]))
            return picked_bytes

        w_codes = deal(nc.vector.tensor_copy, "w_codes", w_raw[:].bitcast(U16), U16)
        x1_scales = pick("x1_scales", xs[:], l1, U8)
        x2_scales = pick("x2_scales", xs[:], l2, U8)
        x1_words = pick("x1_words", x_words[:].bitcast(U32), l1, U32)
        ws = tile("ws", [P, R], U8)
        for t in (0, 2, 1, 3):
            nc.vector.tensor_copy(ws[:, t * P : (t + 1) * P], ws_raw[:, t : R : PACK])
        x2_words = pick("ws_raw", x_words[:].bitcast(U32), l2, U32)

        w2_codes = deal(nc.gpsimd.tensor_copy, "w2_codes", w2_raw[:], I32)
        w2s = deal(nc.gpsimd.tensor_copy, "w2s", w2s_raw[:], U8)

        owner = [nc.vector, nc.vector, nc.scalar, nc.scalar]
        a_sb = [tile("a%d" % t, [P, J], F32)[:] for t in range(PACK)]
        for t in (0, 2, 1, 3):
            a_ps = ps.tile([P, J], F32, name="a_ps%d" % t)
            cols = slice(t * P, (t + 1) * P)
            nc.tensor.matmul_mx(
                out=a_ps[:],
                lhsT=w_codes[:].bitcast(U8)[:, 2 * t * P : 2 * (t + 1) * P].bitcast(E2M1X4), lhsT_scale=ws[:, cols],
                rhs=x1_words[:].bitcast(E5M2X4), rhs_scale=x1_scales[:],
                start=True, stop=True,
            )
            if owner[t] is nc.vector:
                nc.vector.tensor_copy(a_sb[t], a_ps[:])
            else:
                nc.scalar.activation(a_sb[t], a_ps[:], ACT.Copy)
            scatter(owner[t], board[t][:], l3[:], a_sb[t])

        b_ps = [ps.tile([P, PACK, JH], F32, name="b_ps%d" % h) for h in range(HALVES)]
        for h in range(HALVES):
            slots = slice(h * JH, (h + 1) * JH)
            for t in range(PACK):
                cols = slice(t * P, (t + 1) * P)
                nc.tensor.matmul_mx(
                    out=b_ps[h][:, t, :],
                    lhsT=w2_codes[:, cols].bitcast(E4M3X4), lhsT_scale=w2s[:, cols],
                    rhs=x2_words[:, slots].bitcast(E5M2X4), rhs_scale=x2_scales[:, slots],
                    start=True, stop=True,
                )

        hid = []
        for h in range(HALVES):
            picked = tile("picked%d" % h, [P, PACK, JH], F32)
            lcols = slice(h * LIST_COLS // HALVES, (h + 1) * LIST_COLS // HALVES)
            for t in range(PACK):
                gather(owner[t], picked[:, t, :], board[t][:], l4[:, lcols])
            diff = tile("diff%d" % h, [P, PACK, JH], F32)
            nc.vector.tensor_tensor(diff[:], picked[:], b_ps[h][:], ALU.subtract)
            hid.append((diff, tile("hid%d" % h, [P, JH, PACK], BF16)))
        tz_pick = tile("tz_pick", [P, NT, J], F32)
        gather(nc.vector, tz_pick[:, 0, :], tz_sb[0][:], l5[:])
        gather(nc.scalar, tz_pick[:, 1, :], tz_sb[1][:], l5[:])
        for diff, hid_h in hid:
            nc.scalar.activation(
                hid_h[:].rearrange("p (c i) t -> p c t i", i=4), diff[:].rearrange("p t (c i) -> p c t i", i=4), ACT.Abs
            )
        hid = [hid_h for diff, hid_h in hid]

        p_ps = []
        for h in range(HALVES):
            codes = tile("hid_codes%d" % h, [P, JH], U32)
            scales = tile("hid_scales%d" % h, [P, JH], U8)
            nc.vector.quantize_mx(out=codes[:].bitcast(E4M3X4), scales=scales[:], in_=hid[h][:].rearrange("p j t -> p (j t)"))
            p_h = ps.tile([P, NT, JH], F32, name="p_ps%d" % h)
            for u in range(NT):
                nc.tensor.matmul_mx(
                    out=p_h[:, u, :],
                    lhsT=wb_codes[:].bitcast(U8)[:, 2 * u * P : 2 * (u + 1) * P].bitcast(E2M1X4),
                    lhsT_scale=wbs[:, u * P : (u + 1) * P],
                    rhs=codes[:].bitcast(E4M3X4), rhs_scale=scales[:],
                    start=True, stop=True,
                )
            p_ps.append(p_h)

        out_rows = out.rearrange("(u p) j -> p u j", p=P)
        for h in range(HALVES):
            slots = slice(h * JH, (h + 1) * JH)
            y = tile("y%d" % h, [P, NT, JH], F32)
            nc.vector.tensor_tensor(y[:], tz_pick[:, :, slots], p_ps[h][:], ALU.add)
            for u, queue in enumerate((nc.sync, nc.scalar)):
                queue.dma_start(out_rows[:, u, slots], y[:, u, :])
